import numpy as np
import ml_dtypes


def mxq(x, axis, fmt="e4m3"):
    dtype, down = {"e4m3": (ml_dtypes.float8_e4m3fn, 7), "e5m2": (ml_dtypes.float8_e5m2, 14)}[fmt]
    v = np.moveaxis(np.asarray(x, np.float32).astype(ml_dtypes.bfloat16).astype(np.float64), axis, -1)
    blocks = v.reshape(v.shape[:-1] + (-1, 32))
    amax = np.abs(blocks).max(-1, keepdims=True)
    byte = np.maximum(np.where(amax > 0, np.frexp(amax)[1] - 1 + 127, 0) - down, 1)
    scale = np.exp2(byte - 127.0)
    codes = (blocks / scale).astype(np.float32).astype(dtype).astype(np.float64)
    return np.moveaxis((codes * scale).reshape(v.shape), -1, axis)


WIDE = False


def mx_kscale(k):
    if not WIDE:
        return np.ones(k)
    levels = np.array([10, -10, 5, -5, 0])
    if k % 512:
        return np.exp2(np.random.permutation(np.resize(levels, k // 32))).repeat(32)
    a = np.empty((k // 512, 16))
    for p in range(k // 512):
        a[p, :8] = np.random.permutation(np.resize(levels, 8))
        for g in range(8):
            far = levels[np.abs(levels - a[p, g]) >= 10]
            a[p, g + 8] = far[np.random.randint(len(far))]
    return np.exp2(a.ravel()).repeat(32)


def f64(x):
    return np.asarray(x).astype(np.float64)


def striped(idx):
    return np.tile(np.asarray(idx).reshape(-1, 16).T, (8, 1)).astype(np.uint16)


def unstriped(offs):
    return offs[:16].T.reshape(-1).astype(np.int64)


E2M1 = np.array([0.0, 0.5, 1.0, 1.5, 2.0, 3.0, 4.0, 6.0, -0.0, -0.5, -1.0, -1.5, -2.0, -3.0, -4.0, -6.0])


def pack_weight(w, fmt):
    k, n = w.shape
    w = f64(np.asarray(w, np.float32).astype(ml_dtypes.bfloat16)).reshape(k // 32, 32, n)
    amax = np.abs(w).max(1)
    if fmt == "e4m3":
        byte = np.frexp(amax)[1] - 1 + 127 - 7
    else:
        mant, ex = np.frexp(amax / 6.0)
        byte = np.where(mant > 0.5, ex, ex - 1) + 127
    byte = np.clip(np.where(amax > 0, byte, 1), 1, 254)
    scaled = (w * np.exp2(127.0 - byte)[:, None, :]).reshape(k, n).astype(np.float32)
    by_word = np.ascontiguousarray(scaled.reshape(k // 512, 128, 4, n).transpose(0, 1, 3, 2))
    if fmt == "e4m3":
        words = by_word.astype(ml_dtypes.float8_e4m3fn).view(np.uint8)
    else:
        c = by_word.astype(ml_dtypes.float4_e2m1fn).view(np.uint8) & 0xF
        words = (c[..., 0::2] | (c[..., 1::2] << 4)).reshape(k // 512, 128, 2 * n)
    return np.ascontiguousarray(words), np.ascontiguousarray(byte.astype(np.uint8).reshape(k // 512, 16, n))


def unpack_weight(words, scales, fmt):
    g, _, n = scales.shape
    words = np.ascontiguousarray(words).reshape(g, 128, n, -1)
    if fmt == "e4m3":
        vals = words.view(ml_dtypes.float8_e4m3fn).astype(np.float64)
    else:
        nib = np.empty((g, 128, n, 4), np.uint8)
        nib[..., 0::2] = words & 0xF
        nib[..., 1::2] = words >> 4
        vals = E2M1[nib]
    vals = vals * np.repeat(np.exp2(scales.astype(np.float64) - 127.0), 8, axis=1)[..., None]
    return vals.transpose(0, 1, 3, 2).reshape(g * 512, n)


D, T, I, J, U, M = 512, 2048, 512, 512, 1024, 1024


def setup_inputs():
    n = np.random.standard_normal
    idx = np.random.permutation(T)[:I]
    idx2 = np.random.permutation(U)[:J]
    idx3 = np.random.permutation(U)[:J]
    idx4 = np.random.permutation(M)[:J]
    fd = mx_kscale(D)
    keysp = pack_weight(n((D, T)) / fd[:, None], "e4m3")
    return {
        "keys_words": keysp[0],
        "keys_scales": keysp[1],
        "notes": (n((D, U)) * 1.0 / np.sqrt(D) * fd[:, None]).astype(np.float32),
        "old": (1.0 * n((I, M))).astype(np.float32),
        "fade": (np.random.uniform(0.3, 0.9, (I, 1))).astype(np.float32),
        "offs": striped(idx),
        "offs2": striped(idx2),
        "offs3": striped(idx3),
        "offs4": striped(idx4),
    }


def reference(keys_words, keys_scales, notes, old, fade, offs, offs2, offs3, offs4):
    idx = unstriped(offs)
    idx2 = unstriped(offs2)
    idx3 = unstriped(offs3)
    idx4 = unstriped(offs4)
    keysu = unpack_weight(keys_words, keys_scales, "e4m3")
    keysidxg = keysu[:, idx]
    notesq = mxq(f64(notes), 0, "e4m3")
    g1 = keysidxg.T @ notesq
    g0 = g1[:, idx2] * g1[:, idx3]
    gf = np.zeros((I, M))
    gf[:, idx4] = g0
    y = f64(old) * f64(fade) + gf
    return y

@@ -1,0 +1,154 @@
+from contextlib import ExitStack
+
+import concourse.mybir as mybir
+
+D, T, I, J, U, M = 512, 2048, 512, 512, 1024, 1024
+FLOPS = 2 * D * I * U
+
+F32 = mybir.dt.float32
+BF16 = mybir.dt.bfloat16
+I32 = mybir.dt.int32
+U32 = mybir.dt.uint32
+U16 = mybir.dt.uint16
+U8 = mybir.dt.uint8
+FP8X4 = mybir.dt.float8_e4m3fn_x4
+MULT = mybir.AluOpType.mult
+ADD = mybir.AluOpType.add
+COPY = mybir.ActivationFunctionType.Copy
+
+P = 128
+PACK = 4
+ROW_TILES = I // P
+CHUNK = 256
+CHUNKS = U // CHUNK
+HALF = J // 2
+
+
+def tile_attend_tab_lookedtimes_keep_kernel(
+    tc, keys_words, keys_scales, notes, old, fade, offs, offs2, offs3, offs4, out
+):
+    nc = tc.nc
+    with ExitStack() as ctx:
+        keep = ctx.enter_context(tc.tile_pool(name="keep", bufs=1))
+        psum = ctx.enter_context(tc.psum_pool(name="psum", bufs=8))
+
+        token_list = keep.tile([P, I // 16], U16, name="token_list")
+        left_list = keep.tile([P, J // 16], U16, name="left_list")
+        right_list = keep.tile([P, J // 16], U16, name="right_list")
+        place_list = keep.tile([P, J // 16], U16, name="place_list")
+        pool_words = keep.tile([P, T], U32, name="pool_words")
+        pool_scales = keep.tile([P, T], U8, name="pool_scales")
+
+        nc.vector.memset(pool_scales[:].bitcast(I32), 0)
+        landed_scales = keep.tile([P, T // 4], I32, name="landed_scales")
+        nc.sync.dma_start(token_list[:], offs)
+        for r in range(4):
+            nc.sync.dma_start(landed_scales[r:P:32, :], keys_scales[0, r:16:4, :].bitcast(I32))
+        nc.sync.dma_start(
+            pool_words[:].bitcast(I32), keys_words[0].rearrange("p t r -> p (t r)").bitcast(I32)
+        )
+        notes_rows = notes.rearrange("(p j) u -> p j u", j=PACK)
+        raw = []
+        for c in range(CHUNKS):
+            raw.append(keep.tile([P, PACK, CHUNK], F32, name=f"raw{c}"))
+            nc.sync.dma_start(raw[c][:], notes_rows[:, :, c * CHUNK : (c + 1) * CHUNK])
+        nc.sync.dma_start(left_list[:], offs2)
+        nc.sync.dma_start(right_list[:], offs3)
+        nc.sync.dma_start(place_list[:], offs4)
+        fades = keep.tile([P, ROW_TILES], F32, name="fades")
+        with nc.allow_non_contiguous_dma(reason="one fading value for each partition"):
+            nc.sync.dma_start(fades[:], fade.rearrange("(r p) o -> p (r o)", p=P))
+        result = []
+        for r in range(ROW_TILES):
+            result.append(keep.tile([P, M], F32, name=f"result{r}"))
+            nc.sync.dma_start(result[r][:], old[r * P : (r + 1) * P, :])
+
+        windows = []
+        for w in range(3):
+            windows.append(keep.tile([P, M], F32, name=f"window{w}"))
+            nc.vector.memset(windows[w][:], 0.0)
+        placed = [windows[0], windows[1], windows[0], windows[2]]
+
+        key_words = keep.tile([P, I], U32, name="key_words", align_bytes=64)
+        key_scales = keep.tile([P, I], U8, name="key_scales", align_bytes=64)
+        for q in range(4):
+            live = slice(32 * q, 32 * q + 4)
+            nc.vector.tensor_copy(pool_scales[live, :].bitcast(I32), landed_scales[live, :])
+        nc.vector.tensor_copy(key_scales[:], pool_scales[:].indirect(token_list[:]))
+        nc.vector.tensor_copy(key_words[:], pool_words[:].indirect(token_list[:]))
+
+        wide = [keep.tile([P, U], F32, name=f"wide{r}") for r in range(ROW_TILES)]
+        for c in range(CHUNKS):
+            grouped = keep.tile([P, CHUNK, PACK], BF16, name=f"grouped{c}", align_bytes=64)
+            nc.vector.tensor_copy(
+                grouped[:].rearrange("p (a i) j -> p a j i", i=4),
+                raw[c][:].rearrange("p j (a i) -> p a j i", i=4),
+            )
+            note_words = keep.tile([P, CHUNK], U32, name=f"note_words{c}", align_bytes=64)
+            note_scales = keep.tile([P, CHUNK], U8, name=f"note_scales{c}", align_bytes=64)
+            nc.vector.quantize_mx(
+                out=note_words[:].bitcast(FP8X4),
+                scales=note_scales[:],
+                in_=grouped[:].rearrange("p u j -> p (u j)"),
+            )
+            for r in range(ROW_TILES):
+                rows = slice(r * P, (r + 1) * P)
+                acc = psum.tile([P, CHUNK], F32, name="acc")
+                nc.tensor.matmul_mx(
+                    out=acc[:],
+                    lhsT=key_words[:, rows].bitcast(FP8X4),
+                    lhsT_scale=key_scales[:, rows],
+                    rhs=note_words[:].bitcast(FP8X4),
+                    rhs_scale=note_scales[:],
+                    start=True,
+                    stop=True,
+                )
+                nc.scalar.activation(wide[r][:, c * CHUNK : (c + 1) * CHUNK], acc[:], COPY)
+                if c == CHUNKS - 1 and r == 0:
+                    left0 = keep.tile([P, J], F32, name="left0")
+                    nc.scalar.activation(left0[:], wide[0][:].indirect(left_list[:]), COPY)
+
+        left = [left0] + [keep.tile([P, J], F32, name=f"left{r}") for r in range(1, ROW_TILES)]
+        second = [keep.tile([P, J], F32, name=f"second{r}") for r in range(ROW_TILES)]
+
+        def gather_left(r):
+            nc.scalar.activation(left[r][:], wide[r][:].indirect(left_list[:]), COPY)
+
+        def gather_product(r):
+            nc.vector.tensor_tensor(second[r][:], wide[r][:].indirect(right_list[:]), left[r][:], MULT)
+
+        def scatter_product(r):
+            nc.vector.tensor_tensor(placed[r][:].indirect(place_list[:]), left[r][:], second[r][:], MULT)
+
+        def scatter_copy(r):
+            for h in range(2):
+                nc.scalar.activation(
+                    placed[r][:].indirect(place_list[:, h * HALF // 16 : (h + 1) * HALF // 16]),
+                    second[r][:, h * HALF : (h + 1) * HALF],
+                    COPY,
+                )
+
+        def finish(r, pieces):
+            width = M // pieces
+            for h in range(pieces):
+                cols = slice(h * width, (h + 1) * width)
+                nc.vector.scalar_tensor_tensor(
+                    result[r][:, cols], result[r][:, cols], fades[:, r : r + 1], placed[r][:, cols], MULT, ADD
+                )
+                nc.sync.dma_start(out[r * P : (r + 1) * P, cols], result[r][:, cols])
+
+        nc.vector.tensor_copy(second[0][:], wide[0][:].indirect(right_list[:]))
+        scatter_product(0)
+        gather_left(1)
+        gather_left(3)
+        gather_product(1)
+        gather_left(2)
+        finish(0, 1)
+        nc.scalar.activation(second[2][:], wide[2][:].indirect(right_list[:]), COPY)
+        gather_product(3)
+        scatter_copy(1)
+        scatter_product(2)
+        scatter_copy(3)
+        finish(1, 1)
+        finish(2, 1)
+        finish(3, 2)

@@ -36,7 +36,7 @@ def tile_attend_tab_lookedtimes_keep_kernel(
         left_list = keep.tile([P, J // 16], U16, name="left_list")
         right_list = keep.tile([P, J // 16], U16, name="right_list")
         place_list = keep.tile([P, J // 16], U16, name="place_list")
-        pool_words = keep.tile([P, T], U32, name="pool_words")
+        pool_words = keep.tile([P, T], U32, name="pool_words", tag="words_then_notes", align_bytes=64)
         pool_scales = keep.tile([P, T], U8, name="pool_scales")
 
         nc.vector.memset(pool_scales[:].bitcast(I32), 0)
@@ -44,14 +44,15 @@ def tile_attend_tab_lookedtimes_keep_kernel(
         nc.sync.dma_start(token_list[:], offs)
         for r in range(4):
             nc.sync.dma_start(landed_scales[r:P:32, :], keys_scales[0, r:16:4, :].bitcast(I32))
-        nc.sync.dma_start(
-            pool_words[:].bitcast(I32), keys_words[0].rearrange("p t r -> p (t r)").bitcast(I32)
-        )
         notes_rows = notes.rearrange("(p j) u -> p j u", j=PACK)
         raw = []
         for c in range(CHUNKS):
             raw.append(keep.tile([P, PACK, CHUNK], F32, name=f"raw{c}"))
             nc.sync.dma_start(raw[c][:], notes_rows[:, :, c * CHUNK : (c + 1) * CHUNK])
+            if c == 0:
+                nc.sync.dma_start(
+                    pool_words[:].bitcast(I32), keys_words[0].rearrange("p t r -> p (t r)").bitcast(I32)
+                )
         nc.sync.dma_start(left_list[:], offs2)
         nc.sync.dma_start(right_list[:], offs3)
         nc.sync.dma_start(place_list[:], offs4)
@@ -75,12 +76,17 @@ def tile_attend_tab_lookedtimes_keep_kernel(
             live = slice(32 * q, 32 * q + 4)
             nc.vector.tensor_copy(pool_scales[live, :].bitcast(I32), landed_scales[live, :])
         nc.vector.tensor_copy(key_scales[:], pool_scales[:].indirect(token_list[:]))
-        nc.vector.tensor_copy(key_words[:], pool_words[:].indirect(token_list[:]))
 
         wide = [keep.tile([P, U], F32, name=f"wide{r}") for r in range(ROW_TILES)]
-        for c in range(CHUNKS):
-            grouped = keep.tile([P, CHUNK, PACK], BF16, name=f"grouped{c}", align_bytes=64)
-            nc.vector.tensor_copy(
+        left = [keep.tile([P, J], F32, name=f"left{r}") for r in range(ROW_TILES)]
+        second = [keep.tile([P, J], F32, name=f"second{r}") for r in range(ROW_TILES)]
+        sums = {}
+
+        def quantise_and_multiply(c):
+            tag = "words_then_notes" if c == 1 else f"grouped{c}"
+            grouped = keep.tile([P, CHUNK, PACK], BF16, name=f"grouped{c}", tag=tag, align_bytes=64)
+            interleave = nc.scalar.copy if c == 0 else nc.vector.tensor_copy
+            interleave(
                 grouped[:].rearrange("p (a i) j -> p a j i", i=4),
                 raw[c][:].rearrange("p j (a i) -> p a j i", i=4),
             )
@@ -93,9 +99,13 @@ def tile_attend_tab_lookedtimes_keep_kernel(
             )
             for r in range(ROW_TILES):
                 rows = slice(r * P, (r + 1) * P)
-                acc = psum.tile([P, CHUNK], F32, name="acc")
+                if c == 0:
+                    nc.vector.tensor_copy(
+                        key_words[:, rows], pool_words[:].indirect(token_list[:, r * 8 : (r + 1) * 8])
+                    )
+                sums[c, r] = psum.tile([P, CHUNK], F32, name="acc")
                 nc.tensor.matmul_mx(
-                    out=acc[:],
+                    out=sums[c, r][:],
                     lhsT=key_words[:, rows].bitcast(FP8X4),
                     lhsT_scale=key_scales[:, rows],
                     rhs=note_words[:].bitcast(FP8X4),
@@ -103,13 +113,18 @@ def tile_attend_tab_lookedtimes_keep_kernel(
                     start=True,
                     stop=True,
                 )
-                nc.scalar.activation(wide[r][:, c * CHUNK : (c + 1) * CHUNK], acc[:], COPY)
-                if c == CHUNKS - 1 and r == 0:
-                    left0 = keep.tile([P, J], F32, name="left0")
-                    nc.scalar.activation(left0[:], wide[0][:].indirect(left_list[:]), COPY)
 
-        left = [left0] + [keep.tile([P, J], F32, name=f"left{r}") for r in range(1, ROW_TILES)]
-        second = [keep.tile([P, J], F32, name=f"second{r}") for r in range(ROW_TILES)]
+        def empty(c, r):
+            nc.scalar.activation(wide[r][:, c * CHUNK : (c + 1) * CHUNK], sums[c, r][:], COPY)
+
+        for c in range(CHUNKS - 2):
+            quantise_and_multiply(c)
+            for r in range(ROW_TILES):
+                empty(c, r)
+        quantise_and_multiply(CHUNKS - 2)
+        empty(CHUNKS - 2, 0)
+        quantise_and_multiply(CHUNKS - 1)
+        empty(CHUNKS - 1, 0)
 
         def gather_left(r):
             nc.scalar.activation(left[r][:], wide[r][:].indirect(left_list[:]), COPY)
@@ -137,8 +152,12 @@ def tile_attend_tab_lookedtimes_keep_kernel(
                 )
                 nc.sync.dma_start(out[r * P : (r + 1) * P, cols], result[r][:, cols])
 
+        gather_left(0)
         nc.vector.tensor_copy(second[0][:], wide[0][:].indirect(right_list[:]))
         scatter_product(0)
+        for r in (1, 3, 2):
+            empty(CHUNKS - 2, r)
+            empty(CHUNKS - 1, r)
         gather_left(1)
         gather_left(3)
         gather_product(1)
@@ -151,4 +170,4 @@ def tile_attend_tab_lookedtimes_keep_kernel(
         scatter_copy(3)
         finish(1, 1)
         finish(2, 1)
-        finish(3, 2)
+        finish(3, 4)

@@ -30,7 +30,7 @@ def tile_attend_tab_lookedtimes_keep_kernel(
     nc = tc.nc
     with ExitStack() as ctx:
         keep = ctx.enter_context(tc.tile_pool(name="keep", bufs=1))
-        psum = ctx.enter_context(tc.psum_pool(name="psum", bufs=8))
+        psum = ctx.enter_context(tc.psum_pool(name="psum", bufs=1))
 
         token_list = keep.tile([P, I // 16], U16, name="token_list")
         left_list = keep.tile([P, J // 16], U16, name="left_list")
@@ -41,18 +41,24 @@ def tile_attend_tab_lookedtimes_keep_kernel(
 
         nc.vector.memset(pool_scales[:].bitcast(I32), 0)
         landed_scales = keep.tile([P, T // 4], I32, name="landed_scales")
-        nc.sync.dma_start(token_list[:], offs)
-        for r in range(4):
-            nc.sync.dma_start(landed_scales[r:P:32, :], keys_scales[0, r:16:4, :].bitcast(I32))
         notes_rows = notes.rearrange("(p j) u -> p j u", j=PACK)
-        raw = []
-        for c in range(CHUNKS):
-            raw.append(keep.tile([P, PACK, CHUNK], F32, name=f"raw{c}"))
+        raw = [keep.tile([P, PACK, CHUNK], F32, name=f"raw{c}") for c in range(CHUNKS)]
+
+        def load_notes(c):
             nc.sync.dma_start(raw[c][:], notes_rows[:, :, c * CHUNK : (c + 1) * CHUNK])
-            if c == 0:
-                nc.sync.dma_start(
-                    pool_words[:].bitcast(I32), keys_words[0].rearrange("p t r -> p (t r)").bitcast(I32)
-                )
+
+        load_notes(0)
+        nc.sync.dma_start(token_list[:], offs)
+        for q in range(4):
+            nc.sync.dma_start(
+                landed_scales[32 * q : 32 * q + 4, :], keys_scales[0, 4 * q : 4 * q + 4, :].bitcast(I32)
+            )
+        load_notes(1)
+        nc.sync.dma_start(
+            pool_words[:].bitcast(I32), keys_words[0].rearrange("p t r -> p (t r)").bitcast(I32)
+        )
+        load_notes(2)
+        load_notes(3)
         nc.sync.dma_start(left_list[:], offs2)
         nc.sync.dma_start(right_list[:], offs3)
         nc.sync.dma_start(place_list[:], offs4)
@@ -67,10 +73,10 @@ def tile_attend_tab_lookedtimes_keep_kernel(
         windows = []
         for w in range(3):
             windows.append(keep.tile([P, M], F32, name=f"window{w}"))
-            nc.vector.memset(windows[w][:], 0.0)
+            clear = nc.vector.memset if w == 0 else nc.gpsimd.memset
+            clear(windows[w][:], 0.0)
         placed = [windows[0], windows[1], windows[0], windows[2]]
 
-        key_words = keep.tile([P, I], U32, name="key_words", align_bytes=64)
         key_scales = keep.tile([P, I], U8, name="key_scales", align_bytes=64)
         for q in range(4):
             live = slice(32 * q, 32 * q + 4)
@@ -80,51 +86,53 @@ def tile_attend_tab_lookedtimes_keep_kernel(
         wide = [keep.tile([P, U], F32, name=f"wide{r}") for r in range(ROW_TILES)]
         left = [keep.tile([P, J], F32, name=f"left{r}") for r in range(ROW_TILES)]
         second = [keep.tile([P, J], F32, name=f"second{r}") for r in range(ROW_TILES)]
-        sums = {}
+        note_words = keep.tile([P, U], U32, name="note_words", align_bytes=64)
+        note_scales = keep.tile([P, U], U8, name="note_scales", align_bytes=64)
 
-        def quantise_and_multiply(c):
-            tag = "words_then_notes" if c == 1 else f"grouped{c}"
+        def quantise(c, interleave, tag):
+            cols = slice(c * CHUNK, (c + 1) * CHUNK)
             grouped = keep.tile([P, CHUNK, PACK], BF16, name=f"grouped{c}", tag=tag, align_bytes=64)
-            interleave = nc.scalar.copy if c == 0 else nc.vector.tensor_copy
             interleave(
                 grouped[:].rearrange("p (a i) j -> p a j i", i=4),
                 raw[c][:].rearrange("p j (a i) -> p a j i", i=4),
             )
-            note_words = keep.tile([P, CHUNK], U32, name=f"note_words{c}", align_bytes=64)
-            note_scales = keep.tile([P, CHUNK], U8, name=f"note_scales{c}", align_bytes=64)
             nc.vector.quantize_mx(
-                out=note_words[:].bitcast(FP8X4),
-                scales=note_scales[:],
+                out=note_words[:, cols].bitcast(FP8X4),
+                scales=note_scales[:, cols],
                 in_=grouped[:].rearrange("p u j -> p (u j)"),
             )
-            for r in range(ROW_TILES):
-                rows = slice(r * P, (r + 1) * P)
-                if c == 0:
-                    nc.vector.tensor_copy(
-                        key_words[:, rows], pool_words[:].indirect(token_list[:, r * 8 : (r + 1) * 8])
-                    )
-                sums[c, r] = psum.tile([P, CHUNK], F32, name="acc")
-                nc.tensor.matmul_mx(
-                    out=sums[c, r][:],
-                    lhsT=key_words[:, rows].bitcast(FP8X4),
-                    lhsT_scale=key_scales[:, rows],
-                    rhs=note_words[:].bitcast(FP8X4),
-                    rhs_scale=note_scales[:],
-                    start=True,
-                    stop=True,
-                )
 
-        def empty(c, r):
-            nc.scalar.activation(wide[r][:, c * CHUNK : (c + 1) * CHUNK], sums[c, r][:], COPY)
+        def multiply(r, cols, bank):
+            rows = slice(r * P, (r + 1) * P)
+            acc = psum.tile([P, cols.stop - cols.start], F32, name=bank)
+            nc.tensor.matmul_mx(
+                out=acc[:],
+                lhsT=key_words[:, rows].bitcast(FP8X4),
+                lhsT_scale=key_scales[:, rows],
+                rhs=note_words[:, cols].bitcast(FP8X4),
+                rhs_scale=note_scales[:, cols],
+                start=True,
+                stop=True,
+            )
+            return acc
 
-        for c in range(CHUNKS - 2):
-            quantise_and_multiply(c)
-            for r in range(ROW_TILES):
-                empty(c, r)
-        quantise_and_multiply(CHUNKS - 2)
-        empty(CHUNKS - 2, 0)
-        quantise_and_multiply(CHUNKS - 1)
-        empty(CHUNKS - 1, 0)
+        def empty(r, cols, acc):
+            nc.scalar.activation(wide[r][:, cols], acc[:], COPY)
+
+        quantise(0, nc.scalar.copy, "grouped0")
+        quantise(1, nc.scalar.copy, "notes_then_keys")
+        key_words = keep.tile([P, I], U32, name="key_words", tag="notes_then_keys", align_bytes=64)
+        first, third, fourth = slice(0, 2 * CHUNK), slice(2 * CHUNK, 3 * CHUNK), slice(3 * CHUNK, U)
+        for r in range(ROW_TILES):
+            nc.vector.tensor_copy(
+                key_words[:, r * P : (r + 1) * P], pool_words[:].indirect(token_list[:, r * 8 : (r + 1) * 8])
+            )
+            empty(r, first, multiply(r, first, f"bank{r}"))
+        quantise(2, nc.vector.tensor_copy, "words_then_notes")
+        empty(0, third, multiply(0, third, "bank4"))
+        quantise(3, nc.vector.tensor_copy, "grouped3")
+        nc.vector.tensor_copy(wide[0][:, fourth], multiply(0, fourth, "bank5")[:])
+        later = slice(2 * CHUNK, U)
 
         def gather_left(r):
             nc.scalar.activation(left[r][:], wide[r][:].indirect(left_list[:]), COPY)
@@ -155,19 +163,16 @@ def tile_attend_tab_lookedtimes_keep_kernel(
         gather_left(0)
         nc.vector.tensor_copy(second[0][:], wide[0][:].indirect(right_list[:]))
         scatter_product(0)
-        for r in (1, 3, 2):
-            empty(CHUNKS - 2, r)
-            empty(CHUNKS - 1, r)
-        gather_left(1)
-        gather_left(3)
+        for r, bank in ((1, "bank6"), (3, "bank7"), (2, "bank0")):
+            empty(r, later, multiply(r, later, bank))
+            gather_left(r)
         gather_product(1)
-        gather_left(2)
         finish(0, 1)
         nc.scalar.activation(second[2][:], wide[2][:].indirect(right_list[:]), COPY)
         gather_product(3)
         scatter_copy(1)
         scatter_product(2)
         scatter_copy(3)
-        finish(1, 1)
-        finish(2, 1)
-        finish(3, 4)
+        finish(1, 2)
+        finish(2, 2)
+        finish(3, 2)

from contextlib import ExitStack

import concourse.mybir as mybir

D, T, I, J, U, M = 512, 2048, 512, 512, 1024, 1024
FLOPS = 2 * D * I * U

F32 = mybir.dt.float32
BF16 = mybir.dt.bfloat16
I32 = mybir.dt.int32
U32 = mybir.dt.uint32
U16 = mybir.dt.uint16
U8 = mybir.dt.uint8
FP8X4 = mybir.dt.float8_e4m3fn_x4
MULT = mybir.AluOpType.mult
ADD = mybir.AluOpType.add
COPY = mybir.ActivationFunctionType.Copy

P = 128
PACK = 4
ROW_TILES = I // P
CHUNK = 256
CHUNKS = U // CHUNK
HALF = J // 2


def tile_attend_tab_lookedtimes_keep_kernel(
    tc, keys_words, keys_scales, notes, old, fade, offs, offs2, offs3, offs4, out
):
    nc = tc.nc
    with ExitStack() as ctx:
        keep = ctx.enter_context(tc.tile_pool(name="keep", bufs=1))
        psum = ctx.enter_context(tc.psum_pool(name="psum", bufs=1))

        token_list = keep.tile([P, I // 16], U16, name="token_list")
        left_list = keep.tile([P, J // 16], U16, name="left_list")
        right_list = keep.tile([P, J // 16], U16, name="right_list")
        place_list = keep.tile([P, J // 16], U16, name="place_list")
        pool_words = keep.tile([P, T], U32, name="pool_words", tag="words_then_notes", align_bytes=64)
        pool_scales = keep.tile([P, T], U8, name="pool_scales")

        nc.vector.memset(pool_scales[:].bitcast(I32), 0)
        landed_scales = keep.tile([P, T // 4], I32, name="landed_scales")
        notes_rows = notes.rearrange("(p j) u -> p j u", j=PACK)
        raw = [keep.tile([P, PACK, CHUNK], F32, name=f"raw{c}") for c in range(CHUNKS)]

        def load_notes(c):
            nc.sync.dma_start(raw[c][:], notes_rows[:, :, c * CHUNK : (c + 1) * CHUNK])

        load_notes(0)
        nc.sync.dma_start(token_list[:], offs)
        for q in range(4):
            nc.sync.dma_start(
                landed_scales[32 * q : 32 * q + 4, :], keys_scales[0, 4 * q : 4 * q + 4, :].bitcast(I32)
            )
        load_notes(1)
        nc.sync.dma_start(
            pool_words[:].bitcast(I32), keys_words[0].rearrange("p t r -> p (t r)").bitcast(I32)
        )
        load_notes(2)
        load_notes(3)
        nc.sync.dma_start(left_list[:], offs2)
        nc.sync.dma_start(right_list[:], offs3)
        nc.sync.dma_start(place_list[:], offs4)
        fades = keep.tile([P, ROW_TILES], F32, name="fades")
        with nc.allow_non_contiguous_dma(reason="one fading value for each partition"):
            nc.sync.dma_start(fades[:], fade.rearrange("(r p) o -> p (r o)", p=P))
        result = []
        for r in range(ROW_TILES):
            result.append(keep.tile([P, M], F32, name=f"result{r}"))
            nc.sync.dma_start(result[r][:], old[r * P : (r + 1) * P, :])

        windows = []
        for w in range(3):
            windows.append(keep.tile([P, M], F32, name=f"window{w}"))
            clear = nc.vector.memset if w == 0 else nc.gpsimd.memset
            clear(windows[w][:], 0.0)
        placed = [windows[0], windows[1], windows[0], windows[2]]

        key_scales = keep.tile([P, I], U8, name="key_scales", align_bytes=64)
        for q in range(4):
            live = slice(32 * q, 32 * q + 4)
            nc.vector.tensor_copy(pool_scales[live, :].bitcast(I32), landed_scales[live, :])
        nc.vector.tensor_copy(key_scales[:], pool_scales[:].indirect(token_list[:]))

        wide = [keep.tile([P, U], F32, name=f"wide{r}") for r in range(ROW_TILES)]
        left = [keep.tile([P, J], F32, name=f"left{r}") for r in range(ROW_TILES)]
        second = [keep.tile([P, J], F32, name=f"second{r}") for r in range(ROW_TILES)]
        note_words = keep.tile([P, U], U32, name="note_words", align_bytes=64)
        note_scales = keep.tile([P, U], U8, name="note_scales", align_bytes=64)

        def quantise(c, interleave, tag):
            cols = slice(c * CHUNK, (c + 1) * CHUNK)
            grouped = keep.tile([P, CHUNK, PACK], BF16, name=f"grouped{c}", tag=tag, align_bytes=64)
            interleave(
                grouped[:].rearrange("p (a i) j -> p a j i", i=4),
                raw[c][:].rearrange("p j (a i) -> p a j i", i=4),
            )
            nc.vector.quantize_mx(
                out=note_words[:, cols].bitcast(FP8X4),
                scales=note_scales[:, cols],
                in_=grouped[:].rearrange("p u j -> p (u j)"),
            )

        def multiply(r, cols, bank):
            rows = slice(r * P, (r + 1) * P)
            acc = psum.tile([P, cols.stop - cols.start], F32, name=bank)
            nc.tensor.matmul_mx(
                out=acc[:],
                lhsT=key_words[:, rows].bitcast(FP8X4),
                lhsT_scale=key_scales[:, rows],
                rhs=note_words[:, cols].bitcast(FP8X4),
                rhs_scale=note_scales[:, cols],
                start=True,
                stop=True,
            )
            return acc

        def empty(r, cols, acc):
            nc.scalar.activation(wide[r][:, cols], acc[:], COPY)

        quantise(0, nc.scalar.copy, "grouped0")
        quantise(1, nc.scalar.copy, "notes_then_keys")
        key_words = keep.tile([P, I], U32, name="key_words", tag="notes_then_keys", align_bytes=64)
        first, third, fourth = slice(0, 2 * CHUNK), slice(2 * CHUNK, 3 * CHUNK), slice(3 * CHUNK, U)
        for r in range(ROW_TILES):
            nc.vector.tensor_copy(
                key_words[:, r * P : (r + 1) * P], pool_words[:].indirect(token_list[:, r * 8 : (r + 1) * 8])
            )
            empty(r, first, multiply(r, first, f"bank{r}"))
        quantise(2, nc.vector.tensor_copy, "words_then_notes")
        empty(0, third, multiply(0, third, "bank4"))
        quantise(3, nc.vector.tensor_copy, "grouped3")
        nc.vector.tensor_copy(wide[0][:, fourth], multiply(0, fourth, "bank5")[:])
        later = slice(2 * CHUNK, U)

        def gather_left(r):
            nc.scalar.activation(left[r][:], wide[r][:].indirect(left_list[:]), COPY)

        def gather_product(r):
            nc.vector.tensor_tensor(second[r][:], wide[r][:].indirect(right_list[:]), left[r][:], MULT)

        def scatter_product(r):
            nc.vector.tensor_tensor(placed[r][:].indirect(place_list[:]), left[r][:], second[r][:], MULT)

        def scatter_copy(r):
            for h in range(2):
                nc.scalar.activation(
                    placed[r][:].indirect(place_list[:, h * HALF // 16 : (h + 1) * HALF // 16]),
                    second[r][:, h * HALF : (h + 1) * HALF],
                    COPY,
                )

        def finish(r, pieces):
            width = M // pieces
            for h in range(pieces):
                cols = slice(h * width, (h + 1) * width)
                nc.vector.scalar_tensor_tensor(
                    result[r][:, cols], result[r][:, cols], fades[:, r : r + 1], placed[r][:, cols], MULT, ADD
                )
                nc.sync.dma_start(out[r * P : (r + 1) * P, cols], result[r][:, cols])

        gather_left(0)
        nc.vector.tensor_copy(second[0][:], wide[0][:].indirect(right_list[:]))
        scatter_product(0)
        for r, bank in ((1, "bank6"), (3, "bank7"), (2, "bank0")):
            empty(r, later, multiply(r, later, bank))
            gather_left(r)
        gather_product(1)
        finish(0, 1)
        nc.scalar.activation(second[2][:], wide[2][:].indirect(right_list[:]), COPY)
        gather_product(3)
        scatter_copy(1)
        scatter_product(2)
        scatter_copy(3)
        finish(1, 2)
        finish(2, 2)
        finish(3, 2)
